import numpy as np
import ml_dtypes


def mxq(x, axis, fmt="e4m3"):
    dtype, down = {"e4m3": (ml_dtypes.float8_e4m3fn, 7), "e5m2": (ml_dtypes.float8_e5m2, 14)}[fmt]
    v = np.moveaxis(np.asarray(x, np.float32).astype(ml_dtypes.bfloat16).astype(np.float64), axis, -1)
    blocks = v.reshape(v.shape[:-1] + (-1, 32))
    amax = np.abs(blocks).max(-1, keepdims=True)
    byte = np.maximum(np.where(amax > 0, np.frexp(amax)[1] - 1 + 127, 0) - down, 1)
    scale = np.exp2(byte - 127.0)
    codes = (blocks / scale).astype(np.float32).astype(dtype).astype(np.float64)
    return np.moveaxis((codes * scale).reshape(v.shape), -1, axis)


WIDE = False


def mx_kscale(k):
    if not WIDE:
        return np.ones(k)
    levels = np.array([24, -24, 12, -12, 0])
    if k % 512:
        return np.exp2(np.random.permutation(np.resize(levels, k // 32))).repeat(32)
    a = np.empty((k // 512, 16))
    for p in range(k // 512):
        a[p, :8] = np.random.permutation(np.resize(levels, 8))
        for g in range(8):
            far = levels[np.abs(levels - a[p, g]) >= 10]
            a[p, g + 8] = far[np.random.randint(len(far))]
    return np.exp2(a.ravel()).repeat(32)


def f64(x):
    return np.asarray(x).astype(np.float64)


def striped8(idx):
    return np.concatenate([v.reshape(-1, 16).T for v in idx]).astype(np.uint16)


def unstriped8(offs):
    return np.stack([offs[16 * g:16 * g + 16].T.reshape(-1) for g in range(8)]).astype(np.int64)


E2M1 = np.array([0.0, 0.5, 1.0, 1.5, 2.0, 3.0, 4.0, 6.0, -0.0, -0.5, -1.0, -1.5, -2.0, -3.0, -4.0, -6.0])


def pack_weight(w, fmt):
    k, n = w.shape
    w = f64(np.asarray(w, np.float32).astype(ml_dtypes.bfloat16)).reshape(k // 32, 32, n)
    amax = np.abs(w).max(1)
    if fmt == "e4m3":
        byte = np.frexp(amax)[1] - 1 + 127 - 7
    else:
        mant, ex = np.frexp(amax / 6.0)
        byte = np.where(mant > 0.5, ex, ex - 1) + 127
    byte = np.clip(np.where(amax > 0, byte, 1), 1, 254)
    scaled = (w * np.exp2(127.0 - byte)[:, None, :]).reshape(k, n).astype(np.float32)
    by_word = np.ascontiguousarray(scaled.reshape(k // 512, 128, 4, n).transpose(0, 1, 3, 2))
    if fmt == "e4m3":
        words = by_word.astype(ml_dtypes.float8_e4m3fn).view(np.uint8)
    else:
        c = by_word.astype(ml_dtypes.float4_e2m1fn).view(np.uint8) & 0xF
        words = (c[..., 0::2] | (c[..., 1::2] << 4)).reshape(k // 512, 128, 2 * n)
    return np.ascontiguousarray(words), np.ascontiguousarray(byte.astype(np.uint8).reshape(k // 512, 16, n))


def unpack_weight(words, scales, fmt):
    g, _, n = scales.shape
    words = np.ascontiguousarray(words).reshape(g, 128, n, -1)
    if fmt == "e4m3":
        vals = words.view(ml_dtypes.float8_e4m3fn).astype(np.float64)
    else:
        nib = np.empty((g, 128, n, 4), np.uint8)
        nib[..., 0::2] = words & 0xF
        nib[..., 1::2] = words >> 4
        vals = E2M1[nib]
    vals = vals * np.repeat(np.exp2(scales.astype(np.float64) - 127.0), 8, axis=1)[..., None]
    return vals.transpose(0, 1, 3, 2).reshape(g * 512, n)


K, N, T, J = 512, 512, 2048, 512


def setup_inputs():
    n = np.random.standard_normal
    s = mx_kscale(K)[:, None]
    p_w4 = pack_weight(n((K, N)) / np.sqrt(K) / s, "e2m1")
    return {
        "xT": (n((K, T)) * s).astype(np.float32),
        "wgt": np.repeat(np.random.uniform(0.5, 2.0, (8, 3 * J)), 16, axis=0).astype(np.float32),
        "w4_words": p_w4[0],
        "w4_scales": p_w4[1],
        "wd": (0.4 * (n((K, N)) / np.sqrt(K) / s)).astype(np.float32),
        "offs": striped8(np.stack([np.concatenate([np.random.permutation(T)[:J] for _ in range(3)]) for _ in range(8)])),
    }


def reference(xT, wgt, w4_words, w4_scales, wd, offs):
    idx = unstriped8(offs)
    rows = np.arange(K)
    xg = f64(wgt)[rows // 4 % 128] * f64(xT)[rows[:, None], idx[rows % 512 // 64]]
    xT_ = mxq(xg, 0, "e4m3").reshape(K, 3, J)
    w4_ = unpack_weight(w4_words, w4_scales, "e2m1")
    wd_ = mxq(f64(wd), 0, "e4m3")
    a0 = w4_.T @ xT_[:, 0] + wd_.T @ xT_[:, 0]
    a1 = w4_.T @ xT_[:, 1] + wd_.T @ xT_[:, 1]
    a2 = w4_.T @ xT_[:, 2] + wd_.T @ xT_[:, 2]
    return np.maximum(a0, 0.0) + np.maximum(a1, 0.0) + np.maximum(a2, 0.0)

@@ -1,0 +1,206 @@
+from contextlib import ExitStack
+
+import concourse.mybir as mybir
+
+K, N, T, J = 512, 512, 2048, 512
+PICKS = 3
+FLOPS = 2 * 2 * PICKS * K * N * J
+
+F32 = mybir.dt.float32
+BF16 = mybir.dt.bfloat16
+I32 = mybir.dt.int32
+U32 = mybir.dt.uint32
+U16 = mybir.dt.uint16
+U8 = mybir.dt.uint8
+FP8X4 = mybir.dt.float8_e4m3fn_x4
+FP4X4 = mybir.dt.float4_e2m1fn_x4
+MULT = mybir.AluOpType.mult
+ADD = mybir.AluOpType.add
+MAX = mybir.AluOpType.max
+RELU = mybir.ActivationFunctionType.Relu
+
+P = 128
+PACK = 4
+HALF = J // 2
+NT = N // P
+
+
+def tile_list_dl_relus_none_kernel(tc, xT, wgt, w4_words, w4_scales, wd, offs, out):
+    nc = tc.nc
+    with ExitStack() as ctx:
+        keep = ctx.enter_context(tc.tile_pool(name="keep", bufs=1))
+        psum = ctx.enter_context(tc.psum_pool(name="psum", bufs=1))
+
+        offsets = keep.tile([P, PICKS * J // 16], U16, name="offsets")
+        planes = [keep.tile([P, T], F32, name="plane%d" % i) for i in range(PACK)]
+        x_rows = xT.rearrange("(p i) t -> p i t", i=PACK)
+        wd_rows = wd.rearrange("(p i) n -> p i n", i=PACK)
+
+        w4_plane = keep.tile([P, N], U8, name="w4_plane", align_bytes=64)
+        nc.vector.memset(w4_plane[:].bitcast(I32), 0)
+        warm = keep.tile([P, 8], F32, name="warm")
+        nc.vector.memset(warm[:], 0.0)
+        warm2 = keep.tile([P, 8], F32, name="warm2")
+        nc.scalar.activation(warm2[:], warm[:], RELU)
+
+        def load_weights(name, lo, hi):
+            tile = keep.tile([P, hi - lo], F32, name=name)
+            nc.sync.dma_start(tile[:], wgt[:, lo:hi])
+            return tile
+
+        nc.sync.dma_start(planes[0][:], x_rows[:, 0, :])
+        nc.sync.dma_start(offsets[:], offs)
+        wt0 = load_weights("wt0", 0, J)
+        wt1 = load_weights("wt1", J, 2 * J)
+        for i in range(1, PACK):
+            nc.sync.dma_start(planes[i][:], x_rows[:, i, :])
+        w4_codes = keep.tile([P, 2 * N], U8, name="w4_codes", align_bytes=64)
+        nc.sync.dma_start(w4_codes[:].bitcast(I32), w4_words[0].bitcast(I32))
+        for q in range(4):
+            nc.sync.dma_start(w4_plane[32 * q : 32 * q + 4, :].bitcast(I32), w4_scales[0, 4 * q : 4 * q + 4, :].bitcast(I32))
+        wd_raw = []
+        for m in range(2):
+            tile = keep.tile([P, PACK, HALF], F32, name="wd_raw%d" % m)
+            nc.sync.dma_start(tile[:], wd_rows[:, :, m * HALF : (m + 1) * HALF])
+            wd_raw.append(tile)
+        wt2 = [load_weights("wt2%d" % h, 2 * J + h * HALF, 2 * J + (h + 1) * HALF) for h in range(2)]
+
+        def gather(dst, i, first, weights):
+            width = dst.shape[2]
+            nc.vector.tensor_tensor(
+                dst[:, i, :], planes[i][:].indirect(offsets[:, first // 16 : (first + width) // 16]), weights, MULT
+            )
+
+        def weave(dst, src):
+            nc.scalar.copy(
+                dst.rearrange("p (c i) t -> p c t i", i=4), src.rearrange("p t (c i) -> p c t i", i=4)
+            )
+
+        def quantise(codes, scales, woven):
+            nc.vector.quantize_mx(out=codes.bitcast(FP8X4), scales=scales, in_=woven.rearrange("p j t -> p (j t)"))
+
+        def operand(name, width, tag=None):
+            woven = keep.tile([P, width, PACK], BF16, name=name + "_woven", tag=tag or name + "_woven", align_bytes=64)
+            codes = keep.tile([P, width], U32, name=name + "_codes", align_bytes=64)
+            scales = keep.tile([P, width], U8, name=name + "_scales", align_bytes=64)
+            return woven, codes, scales
+
+        g0_all = keep.tile([P, PACK, J], F32, name="g0_all")
+        g1 = keep.tile([P, PACK, J], F32, name="g1")
+        for i in range(PACK):
+            if i < PACK - 1:
+                gather(g0_all, i, 0, wt0[:])
+            else:
+                for h in range(2):
+                    nc.vector.tensor_tensor(
+                        g0_all[:, i, h * HALF : (h + 1) * HALF],
+                        planes[i][:].indirect(offsets[:, h * HALF // 16 : (h + 1) * HALF // 16]),
+                        wt0[:, h * HALF : (h + 1) * HALF],
+                        MULT,
+                    )
+            gather(g1, i, J, wt1[:])
+
+        x0_codes = keep.tile([P, J], U32, name="x0_codes", align_bytes=64)
+        x0_scales = keep.tile([P, J], U8, name="x0_scales", align_bytes=64)
+        for h in range(2):
+            woven = keep.tile([P, HALF, PACK], BF16, name="x0_woven%d" % h, align_bytes=64)
+            cols = slice(h * HALF, (h + 1) * HALF)
+            weave(woven[:], g0_all[:, :, cols])
+            quantise(x0_codes[:, cols], x0_scales[:, cols], woven[:])
+
+        def pass_w4(acc, n, codes, scales, start, stop):
+            nc.tensor.matmul_mx(
+                out=acc, lhsT=w4_codes[:, 2 * P * n : 2 * P * (n + 1)].bitcast(FP4X4), lhsT_scale=w4_plane[:, P * n : P * (n + 1)],
+                rhs=codes.bitcast(FP8X4), rhs_scale=scales, start=start, stop=stop,
+            )
+
+        def pass_wd(acc, n, codes, scales, start, stop):
+            cols = slice(P * (n % 2), P * (n % 2 + 1))
+            nc.tensor.matmul_mx(
+                out=acc, lhsT=wdq[n // 2][1][:, cols].bitcast(FP8X4), lhsT_scale=wdq[n // 2][2][:, cols],
+                rhs=codes.bitcast(FP8X4), rhs_scale=scales, start=start, stop=stop,
+            )
+
+        acc0 = [psum.tile([P, J], F32, name="acc0%d" % n, tag="bank%d" % n) for n in range(NT)]
+        acc1 = [psum.tile([P, J], F32, name="acc1%d" % n, tag="bank%d" % (NT + n)) for n in range(NT)]
+        for n in range(NT):
+            pass_w4(acc0[n][:], n, x0_codes[:], x0_scales[:], True, False)
+
+        wdq = [operand("wd0", HALF, "shared0"), operand("wd1", HALF)]
+        weave(wdq[0][0][:], wd_raw[0][:])
+
+        g2a = keep.tile([P, PACK, HALF], F32, name="g2a")
+        for i in range(PACK):
+            gather(g2a, i, 2 * J, wt2[0][:])
+        quantise(wdq[0][1][:], wdq[0][2][:], wdq[0][0][:])
+        for n in range(2):
+            pass_wd(acc0[n][:], n, x0_codes[:], x0_scales[:], False, True)
+
+        x1 = operand("x1", J)
+        weave(x1[0][:], g1[:])
+        g2b = keep.tile([P, PACK, HALF], F32, name="g2b", tag="shared0", align_bytes=64)
+        for i in range(PACK):
+            gather(g2b, i, 2 * J + HALF, wt2[1][:])
+        quantise(x1[1][:], x1[2][:], x1[0][:])
+        for n in range(NT):
+            pass_w4(acc1[n][:], n, x1[1][:], x1[2][:], True, False)
+        for n in range(2):
+            pass_wd(acc1[n][:], n, x1[1][:], x1[2][:], False, True)
+
+        weave(wdq[1][0][:], wd_raw[1][:])
+        quantise(wdq[1][1][:], wdq[1][2][:], wdq[1][0][:])
+        for n in range(2, NT):
+            pass_wd(acc0[n][:], n, x0_codes[:], x0_scales[:], False, True)
+        for n in range(2, NT):
+            pass_wd(acc1[n][:], n, x1[1][:], x1[2][:], False, True)
+
+        x2a = operand("x2a", HALF)
+        weave(x2a[0][:], g2a[:])
+        quantise(x2a[1][:], x2a[2][:], x2a[0][:])
+
+        r0 = [keep.tile([P, 2, J], F32, name="r0%d" % m) for m in range(2)]
+        r1 = [keep.tile([P, 2, J], F32, name="r1%d" % m) for m in range(2)]
+
+        def relu0(n):
+            nc.scalar.activation(r0[n // 2][:, n % 2, :], acc0[n][:], RELU)
+
+        def add1(n):
+            nc.vector.scalar_tensor_tensor(r1[n // 2][:, n % 2, :], acc1[n][:], 0.0, r0[n // 2][:, n % 2, :], MAX, ADD)
+
+        def project2(x2, banks):
+            accs = []
+            for m in range(2):
+                acc = psum.tile([P, 2, HALF], F32, name="acc2%d" % banks[m], tag="bank%d" % banks[m])
+                for u in range(2):
+                    for b in range(2):
+                        cols = slice(P * b, P * (b + 1))
+                        pass_w4(acc[:, u, cols], 2 * m + u, x2[1][:, cols], x2[2][:, cols], True, False)
+                        pass_wd(acc[:, u, cols], 2 * m + u, x2[1][:, cols], x2[2][:, cols], False, True)
+                accs.append(acc)
+            return accs
+
+        out_rows = out.rearrange("(m u p) j -> p m u j", p=P, u=2)
+
+        def finish(acc, m, h):
+            cols = slice(h * HALF, (h + 1) * HALF)
+            res = keep.tile([P, 2, HALF], F32, name="res%d%d" % (m, h))
+            nc.vector.scalar_tensor_tensor(res[:], acc[:], 0.0, r1[m][:, :, cols], MAX, ADD)
+            nc.sync.dma_start(out_rows[:, m, :, cols], res[:])
+
+        relu0(0)
+        relu0(1)
+        acc2a = project2(x2a, (0, 1))
+        add1(0)
+        add1(1)
+        x2b = operand("x2b", HALF)
+        weave(x2b[0][:], g2b[:])
+        quantise(x2b[1][:], x2b[2][:], x2b[0][:])
+        acc2b = project2(x2b, (NT, NT + 1))
+        relu0(2)
+        relu0(3)
+        finish(acc2a[0], 0, 0)
+        add1(2)
+        add1(3)
+        finish(acc2b[0], 0, 1)
+        finish(acc2a[1], 1, 0)
+        finish(acc2b[1], 1, 1)

@@ -1,6 +1,7 @@
 from contextlib import ExitStack
 
 import concourse.mybir as mybir
+from concourse.masks import make_identity
 
 K, N, T, J = 512, 512, 2048, 512
 PICKS = 3
@@ -43,15 +44,15 @@ def tile_list_dl_relus_none_kernel(tc, xT, wgt, w4_words, w4_scales, wd, offs, o
         warm2 = keep.tile([P, 8], F32, name="warm2")
         nc.scalar.activation(warm2[:], warm[:], RELU)
 
-        def load_weights(name, lo, hi):
-            tile = keep.tile([P, hi - lo], F32, name=name)
-            nc.sync.dma_start(tile[:], wgt[:, lo:hi])
-            return tile
+        ident = keep.tile([P, P], F32, name="ident")
+        make_identity(nc, ident[:])
 
+        rows = keep.tile([P, P], F32, name="rows")
+        nc.sync.dma_start(
+            rows[:], wgt.rearrange("(g r) m -> g (r m)", r=16)[:, 0 : 16 * P].rearrange("g (b f) -> b g f", f=P)
+        )
         nc.sync.dma_start(planes[0][:], x_rows[:, 0, :])
         nc.sync.dma_start(offsets[:], offs)
-        wt0 = load_weights("wt0", 0, J)
-        wt1 = load_weights("wt1", J, 2 * J)
         for i in range(1, PACK):
             nc.sync.dma_start(planes[i][:], x_rows[:, i, :])
         w4_codes = keep.tile([P, 2 * N], U8, name="w4_codes", align_bytes=64)
@@ -63,12 +64,34 @@ def tile_list_dl_relus_none_kernel(tc, xT, wgt, w4_words, w4_scales, wd, offs, o
             tile = keep.tile([P, PACK, HALF], F32, name="wd_raw%d" % m)
             nc.sync.dma_start(tile[:], wd_rows[:, :, m * HALF : (m + 1) * HALF])
             wd_raw.append(tile)
-        wt2 = [load_weights("wt2%d" % h, 2 * J + h * HALF, 2 * J + (h + 1) * HALF) for h in range(2)]
+
+        turned = psum.tile([P, P], F32, name="turned", tag="bank7")
+        nc.tensor.transpose(turned[:], rows[:], ident[:])
+
+        def spread(copy, dst, first, bank):
+            blocks = dst.shape[1] // P
+            wide = keep.tile([P, blocks * P], F32, name="wide%d" % bank)
+            src = turned[:, first // 16 : first // 16 + 8 * blocks]
+            copy(wide[:].rearrange("f (c r) -> f c r", r=16), src.unsqueeze(2).to_broadcast([P, 8 * blocks, 16]))
+            back = psum.tile([P, blocks * P], F32, name="back%d" % bank, tag="bank%d" % bank)
+            for b in range(blocks):
+                nc.tensor.transpose(back[:, b * P : (b + 1) * P], wide[:, b * P : (b + 1) * P], ident[:])
+            copy(dst, back[:])
+
+        g1_flat = keep.tile([P, PACK * J], F32, name="g1_flat")
+        g1 = g1_flat[:].rearrange("p (t j) -> p t j", t=PACK)
+        wt0 = g1_flat[:, 2 * J + HALF : 3 * J + HALF]
+        wt1 = keep.tile([P, J], F32, name="wt1")
+        wt2 = keep.tile([P, J], F32, name="wt2")
+        spread(nc.vector.tensor_copy, wt0[:, 0:HALF], 0, 0)
+        spread(nc.scalar.copy, wt0[:, HALF:J], HALF, 1)
+        spread(nc.scalar.copy, wt1[:], J, 2)
+        spread(nc.scalar.copy, wt2[:], 2 * J, 3)
 
         def gather(dst, i, first, weights):
-            width = dst.shape[2]
+            width = dst.shape[1]
             nc.vector.tensor_tensor(
-                dst[:, i, :], planes[i][:].indirect(offsets[:, first // 16 : (first + width) // 16]), weights, MULT
+                dst, planes[i][:].indirect(offsets[:, first // 16 : (first + width) // 16]), weights, MULT
             )
 
         def weave(dst, src):
@@ -85,25 +108,24 @@ def tile_list_dl_relus_none_kernel(tc, xT, wgt, w4_words, w4_scales, wd, offs, o
             scales = keep.tile([P, width], U8, name=name + "_scales", align_bytes=64)
             return woven, codes, scales
 
+        lo, hi = slice(0, HALF), slice(HALF, J)
         g0_all = keep.tile([P, PACK, J], F32, name="g0_all")
-        g1 = keep.tile([P, PACK, J], F32, name="g1")
-        for i in range(PACK):
-            if i < PACK - 1:
-                gather(g0_all, i, 0, wt0[:])
-            else:
-                for h in range(2):
-                    nc.vector.tensor_tensor(
-                        g0_all[:, i, h * HALF : (h + 1) * HALF],
-                        planes[i][:].indirect(offsets[:, h * HALF // 16 : (h + 1) * HALF // 16]),
-                        wt0[:, h * HALF : (h + 1) * HALF],
-                        MULT,
-                    )
-            gather(g1, i, J, wt1[:])
+        gather(g0_all[:, 0, lo], 0, 0, wt0[:, lo])
+        gather(g0_all[:, 0, hi], 0, HALF, wt0[:, hi])
+        gather(g1[:, 0, :], 0, J, wt1[:])
+        gather(g0_all[:, 1, :], 1, 0, wt0)
+        gather(g1[:, 1, :], 1, J, wt1[:])
+        gather(g0_all[:, 2, :], 2, 0, wt0)
+        gather(g1[:, 2, lo], 2, J, wt1[:, lo])
+        gather(g0_all[:, 3, lo], 3, 0, wt0[:, lo])
+        gather(g0_all[:, 3, hi], 3, HALF, wt0[:, hi])
+        gather(g1[:, 2, hi], 2, J + HALF, wt1[:, hi])
+        gather(g1[:, 3, :], 3, J, wt1[:])
 
         x0_codes = keep.tile([P, J], U32, name="x0_codes", align_bytes=64)
         x0_scales = keep.tile([P, J], U8, name="x0_scales", align_bytes=64)
         for h in range(2):
-            woven = keep.tile([P, HALF, PACK], BF16, name="x0_woven%d" % h, align_bytes=64)
+            woven = keep.tile([P, HALF, PACK], BF16, name="x0_woven%d" % h, tag="x0_woven%d" % h, align_bytes=64)
             cols = slice(h * HALF, (h + 1) * HALF)
             weave(woven[:], g0_all[:, :, cols])
             quantise(x0_codes[:, cols], x0_scales[:, cols], woven[:])
@@ -126,21 +148,18 @@ def tile_list_dl_relus_none_kernel(tc, xT, wgt, w4_words, w4_scales, wd, offs, o
         for n in range(NT):
             pass_w4(acc0[n][:], n, x0_codes[:], x0_scales[:], True, False)
 
-        wdq = [operand("wd0", HALF, "shared0"), operand("wd1", HALF)]
+        wdq = [operand("wd0", HALF), operand("wd1", HALF)]
         weave(wdq[0][0][:], wd_raw[0][:])
-
-        g2a = keep.tile([P, PACK, HALF], F32, name="g2a")
-        for i in range(PACK):
-            gather(g2a, i, 2 * J, wt2[0][:])
         quantise(wdq[0][1][:], wdq[0][2][:], wdq[0][0][:])
+
+        g2a = keep.tile([P, PACK, HALF], F32, name="g2a", tag="x0_woven1", align_bytes=64)
+        for i in range(PACK):
+            gather(g2a[:, i, :], i, 2 * J, wt2[:, lo])
         for n in range(2):
             pass_wd(acc0[n][:], n, x0_codes[:], x0_scales[:], False, True)
 
         x1 = operand("x1", J)
-        weave(x1[0][:], g1[:])
-        g2b = keep.tile([P, PACK, HALF], F32, name="g2b", tag="shared0", align_bytes=64)
-        for i in range(PACK):
-            gather(g2b, i, 2 * J + HALF, wt2[1][:])
+        weave(x1[0][:], g1)
         quantise(x1[1][:], x1[2][:], x1[0][:])
         for n in range(NT):
             pass_w4(acc1[n][:], n, x1[1][:], x1[2][:], True, False)
@@ -149,6 +168,9 @@ def tile_list_dl_relus_none_kernel(tc, xT, wgt, w4_words, w4_scales, wd, offs, o
 
         weave(wdq[1][0][:], wd_raw[1][:])
         quantise(wdq[1][1][:], wdq[1][2][:], wdq[1][0][:])
+        g2b = keep.tile([P, PACK, HALF], F32, name="g2b", tag="x1_woven", align_bytes=64)
+        for i in range(PACK):
+            gather(g2b[:, i, :], i, 2 * J + HALF, wt2[:, hi])
         for n in range(2, NT):
             pass_wd(acc0[n][:], n, x0_codes[:], x0_scales[:], False, True)
         for n in range(2, NT):
@@ -181,14 +203,16 @@ def tile_list_dl_relus_none_kernel(tc, xT, wgt, w4_words, w4_scales, wd, offs, o
 
         out_rows = out.rearrange("(m u p) j -> p m u j", p=P, u=2)
 
-        def finish(acc, m, h):
+        def finish(acc, m, h, tiles=slice(0, 2), tag=None):
             cols = slice(h * HALF, (h + 1) * HALF)
-            res = keep.tile([P, 2, HALF], F32, name="res%d%d" % (m, h))
-            nc.vector.scalar_tensor_tensor(res[:], acc[:], 0.0, r1[m][:, :, cols], MAX, ADD)
-            nc.sync.dma_start(out_rows[:, m, :, cols], res[:])
+            name = "res%d%d%d" % (m, h, tiles.start)
+            res = keep.tile([P, tiles.stop - tiles.start, HALF], F32, name=name, tag=tag or name, align_bytes=64)
+            nc.vector.scalar_tensor_tensor(res[:], acc[:, tiles, :], 0.0, r1[m][:, tiles, cols], MAX, ADD)
+            nc.sync.dma_start(out_rows[:, m, tiles, cols], res[:])
 
         relu0(0)
         relu0(1)
+        relu0(2)
         acc2a = project2(x2a, (0, 1))
         add1(0)
         add1(1)
@@ -196,11 +220,11 @@ def tile_list_dl_relus_none_kernel(tc, xT, wgt, w4_words, w4_scales, wd, offs, o
         weave(x2b[0][:], g2b[:])
         quantise(x2b[1][:], x2b[2][:], x2b[0][:])
         acc2b = project2(x2b, (NT, NT + 1))
-        relu0(2)
         relu0(3)
-        finish(acc2a[0], 0, 0)
         add1(2)
+        finish(acc2a[0], 0, 0, tag="x2b_woven")
         add1(3)
-        finish(acc2b[0], 0, 1)
         finish(acc2a[1], 1, 0)
-        finish(acc2b[1], 1, 1)
+        finish(acc2b[0], 0, 1)
+        finish(acc2b[1], 1, 1, slice(0, 1))
+        finish(acc2b[1], 1, 1, slice(1, 2))

@@ -19,6 +19,7 @@ MULT = mybir.AluOpType.mult
 ADD = mybir.AluOpType.add
 MAX = mybir.AluOpType.max
 RELU = mybir.ActivationFunctionType.Relu
+IDENTITY = mybir.ActivationFunctionType.Identity
 
 P = 128
 PACK = 4
@@ -39,10 +40,6 @@ def tile_list_dl_relus_none_kernel(tc, xT, wgt, w4_words, w4_scales, wd, offs, o
 
         w4_plane = keep.tile([P, N], U8, name="w4_plane", align_bytes=64)
         nc.vector.memset(w4_plane[:].bitcast(I32), 0)
-        warm = keep.tile([P, 8], F32, name="warm")
-        nc.vector.memset(warm[:], 0.0)
-        warm2 = keep.tile([P, 8], F32, name="warm2")
-        nc.scalar.activation(warm2[:], warm[:], RELU)
 
         ident = keep.tile([P, P], F32, name="ident")
         make_identity(nc, ident[:])
@@ -53,24 +50,26 @@ def tile_list_dl_relus_none_kernel(tc, xT, wgt, w4_words, w4_scales, wd, offs, o
         )
         nc.sync.dma_start(planes[0][:], x_rows[:, 0, :])
         nc.sync.dma_start(offsets[:], offs)
-        for i in range(1, PACK):
-            nc.sync.dma_start(planes[i][:], x_rows[:, i, :])
+        wd_raw = [keep.tile([P, PACK, HALF], F32, name="wd_raw%d" % m) for m in range(2)]
+        nc.sync.dma_start(planes[1][:], x_rows[:, 1, :])
+        nc.sync.dma_start(planes[2][:], x_rows[:, 2, :])
+        nc.sync.dma_start(wd_raw[0][:], wd_rows[:, :, 0:HALF])
+        nc.sync.dma_start(planes[3][:], x_rows[:, 3, :])
         w4_codes = keep.tile([P, 2 * N], U8, name="w4_codes", align_bytes=64)
         nc.sync.dma_start(w4_codes[:].bitcast(I32), w4_words[0].bitcast(I32))
         for q in range(4):
             nc.sync.dma_start(w4_plane[32 * q : 32 * q + 4, :].bitcast(I32), w4_scales[0, 4 * q : 4 * q + 4, :].bitcast(I32))
-        wd_raw = []
-        for m in range(2):
-            tile = keep.tile([P, PACK, HALF], F32, name="wd_raw%d" % m)
-            nc.sync.dma_start(tile[:], wd_rows[:, :, m * HALF : (m + 1) * HALF])
-            wd_raw.append(tile)
+        nc.sync.dma_start(wd_raw[1][:], wd_rows[:, :, HALF:N])
 
         turned = psum.tile([P, P], F32, name="turned", tag="bank7")
         nc.tensor.transpose(turned[:], rows[:], ident[:])
 
+        def scalar_identity(dst, src):
+            nc.scalar.activation(dst, src, IDENTITY)
+
         def spread(copy, dst, first, bank):
             blocks = dst.shape[1] // P
-            wide = keep.tile([P, blocks * P], F32, name="wide%d" % bank)
+            wide = keep.tile([P, blocks * P], F32, name="wide%d" % bank, align_bytes=64)
             src = turned[:, first // 16 : first // 16 + 8 * blocks]
             copy(wide[:].rearrange("f (c r) -> f c r", r=16), src.unsqueeze(2).to_broadcast([P, 8 * blocks, 16]))
             back = psum.tile([P, blocks * P], F32, name="back%d" % bank, tag="bank%d" % bank)
@@ -78,13 +77,11 @@ def tile_list_dl_relus_none_kernel(tc, xT, wgt, w4_words, w4_scales, wd, offs, o
                 nc.tensor.transpose(back[:, b * P : (b + 1) * P], wide[:, b * P : (b + 1) * P], ident[:])
             copy(dst, back[:])
 
-        g1_flat = keep.tile([P, PACK * J], F32, name="g1_flat")
-        g1 = g1_flat[:].rearrange("p (t j) -> p t j", t=PACK)
-        wt0 = g1_flat[:, 2 * J + HALF : 3 * J + HALF]
+        wt0 = keep.tile([P, J], F32, name="wt0", align_bytes=64)
         wt1 = keep.tile([P, J], F32, name="wt1")
         wt2 = keep.tile([P, J], F32, name="wt2")
         spread(nc.vector.tensor_copy, wt0[:, 0:HALF], 0, 0)
-        spread(nc.scalar.copy, wt0[:, HALF:J], HALF, 1)
+        spread(scalar_identity, wt0[:, HALF:J], HALF, 1)
         spread(nc.scalar.copy, wt1[:], J, 2)
         spread(nc.scalar.copy, wt2[:], 2 * J, 3)
 
@@ -103,32 +100,37 @@ def tile_list_dl_relus_none_kernel(tc, xT, wgt, w4_words, w4_scales, wd, offs, o
             nc.vector.quantize_mx(out=codes.bitcast(FP8X4), scales=scales, in_=woven.rearrange("p j t -> p (j t)"))
 
         def operand(name, width, tag=None):
-            woven = keep.tile([P, width, PACK], BF16, name=name + "_woven", tag=tag or name + "_woven", align_bytes=64)
-            codes = keep.tile([P, width], U32, name=name + "_codes", align_bytes=64)
+            codes = keep.tile([P, width], U32, name=name + "_codes", tag=tag or name + "_codes", align_bytes=64)
             scales = keep.tile([P, width], U8, name=name + "_scales", align_bytes=64)
-            return woven, codes, scales
+            return codes, scales
+
+        def prepare(name, dst, cols, src):
+            woven = keep.tile([P, HALF, PACK], BF16, name=name, align_bytes=64)
+            weave(woven[:], src)
+            quantise(dst[0][:, cols], dst[1][:, cols], woven[:])
 
         lo, hi = slice(0, HALF), slice(HALF, J)
-        g0_all = keep.tile([P, PACK, J], F32, name="g0_all")
-        gather(g0_all[:, 0, lo], 0, 0, wt0[:, lo])
-        gather(g0_all[:, 0, hi], 0, HALF, wt0[:, hi])
-        gather(g1[:, 0, :], 0, J, wt1[:])
-        gather(g0_all[:, 1, :], 1, 0, wt0)
-        gather(g1[:, 1, :], 1, J, wt1[:])
-        gather(g0_all[:, 2, :], 2, 0, wt0)
-        gather(g1[:, 2, lo], 2, J, wt1[:, lo])
-        gather(g0_all[:, 3, lo], 3, 0, wt0[:, lo])
-        gather(g0_all[:, 3, hi], 3, HALF, wt0[:, hi])
-        gather(g1[:, 2, hi], 2, J + HALF, wt1[:, hi])
-        gather(g1[:, 3, :], 3, J, wt1[:])
+        stage0 = keep.tile([P, PACK * J], F32, name="stage0")
+        stage1 = keep.tile([P, PACK * J], F32, name="stage1")
+        g0 = stage0[:].rearrange("p (t j) -> p t j", t=PACK)
+        g1 = stage1[:].rearrange("p (t j) -> p t j", t=PACK)
+        g2 = [s[:, 0 : PACK * HALF].rearrange("p (t j) -> p t j", t=PACK) for s in (stage0, stage1)]
+        x0, x1 = operand("x0", J), operand("x1", J)
+        x2 = [operand("x2%d" % h, HALF) for h in range(2)]
 
-        x0_codes = keep.tile([P, J], U32, name="x0_codes", align_bytes=64)
-        x0_scales = keep.tile([P, J], U8, name="x0_scales", align_bytes=64)
-        for h in range(2):
-            woven = keep.tile([P, HALF, PACK], BF16, name="x0_woven%d" % h, tag="x0_woven%d" % h, align_bytes=64)
-            cols = slice(h * HALF, (h + 1) * HALF)
-            weave(woven[:], g0_all[:, :, cols])
-            quantise(x0_codes[:, cols], x0_scales[:, cols], woven[:])
+        gather(g0[:, 0, lo], 0, 0, wt0[:, lo])
+        gather(g0[:, 0, hi], 0, HALF, wt0[:, hi])
+        gather(g1[:, 0, :], 0, J, wt1[:])
+        for i in (1, 2):
+            gather(g0[:, i, :], i, 0, wt0[:])
+            gather(g1[:, i, :], i, J, wt1[:])
+        wd_woven0 = keep.tile([P, HALF, PACK], BF16, name="wd_woven0", tag="wide3", align_bytes=64)
+        weave(wd_woven0[:], wd_raw[0][:])
+        gather(g0[:, 3, lo], 3, 0, wt0[:, lo])
+        gather(g0[:, 3, hi], 3, HALF, wt0[:, hi])
+        gather(g1[:, 3, :], 3, J, wt1[:])
+        wdq = [operand("wd0", HALF, "wt0"), operand("wd1", HALF)]
+        quantise(wdq[0][0][:], wdq[0][1][:], wd_woven0[:])
 
         def pass_w4(acc, n, codes, scales, start, stop):
             nc.tensor.matmul_mx(
@@ -139,46 +141,40 @@ def tile_list_dl_relus_none_kernel(tc, xT, wgt, w4_words, w4_scales, wd, offs, o
         def pass_wd(acc, n, codes, scales, start, stop):
             cols = slice(P * (n % 2), P * (n % 2 + 1))
             nc.tensor.matmul_mx(
-                out=acc, lhsT=wdq[n // 2][1][:, cols].bitcast(FP8X4), lhsT_scale=wdq[n // 2][2][:, cols],
+                out=acc, lhsT=wdq[n // 2][0][:, cols].bitcast(FP8X4), lhsT_scale=wdq[n // 2][1][:, cols],
                 rhs=codes.bitcast(FP8X4), rhs_scale=scales, start=start, stop=stop,
             )
 
         acc0 = [psum.tile([P, J], F32, name="acc0%d" % n, tag="bank%d" % n) for n in range(NT)]
         acc1 = [psum.tile([P, J], F32, name="acc1%d" % n, tag="bank%d" % (NT + n)) for n in range(NT)]
-        for n in range(NT):
-            pass_w4(acc0[n][:], n, x0_codes[:], x0_scales[:], True, False)
 
-        wdq = [operand("wd0", HALF), operand("wd1", HALF)]
-        weave(wdq[0][0][:], wd_raw[0][:])
-        quantise(wdq[0][1][:], wdq[0][2][:], wdq[0][0][:])
+        def project(acc, n, x, first, start, stop):
+            cols = slice(first, first + HALF)
+            pass_wd(acc, n, x[0][:, cols], x[1][:, cols], start, False)
+            for b in range(2):
+                cols = slice(first + P * b, first + P * (b + 1))
+                pass_w4(acc[:, P * b : P * (b + 1)], n, x[0][:, cols], x[1][:, cols], False, stop and b == 1)
 
-        g2a = keep.tile([P, PACK, HALF], F32, name="g2a", tag="x0_woven1", align_bytes=64)
-        for i in range(PACK):
-            gather(g2a[:, i, :], i, 2 * J, wt2[:, lo])
-        for n in range(2):
-            pass_wd(acc0[n][:], n, x0_codes[:], x0_scales[:], False, True)
+        def project_half(accs, x, h, tiles):
+            for n in tiles:
+                project(accs[n][:, h * HALF : (h + 1) * HALF], n, x, h * HALF, h == 0, h == 1)
 
-        x1 = operand("x1", J)
-        weave(x1[0][:], g1)
-        quantise(x1[1][:], x1[2][:], x1[0][:])
-        for n in range(NT):
-            pass_w4(acc1[n][:], n, x1[1][:], x1[2][:], True, False)
-        for n in range(2):
-            pass_wd(acc1[n][:], n, x1[1][:], x1[2][:], False, True)
-
-        weave(wdq[1][0][:], wd_raw[1][:])
-        quantise(wdq[1][1][:], wdq[1][2][:], wdq[1][0][:])
-        g2b = keep.tile([P, PACK, HALF], F32, name="g2b", tag="x1_woven", align_bytes=64)
-        for i in range(PACK):
-            gather(g2b[:, i, :], i, 2 * J + HALF, wt2[:, hi])
-        for n in range(2, NT):
-            pass_wd(acc0[n][:], n, x0_codes[:], x0_scales[:], False, True)
-        for n in range(2, NT):
-            pass_wd(acc1[n][:], n, x1[1][:], x1[2][:], False, True)
-
-        x2a = operand("x2a", HALF)
-        weave(x2a[0][:], g2a[:])
-        quantise(x2a[1][:], x2a[2][:], x2a[0][:])
+        prepare("x0_woven0", x0, lo, g0[:, :, lo])
+        project_half(acc0, x0, 0, (0, 1))
+        prepare("x0_woven1", x0, hi, g0[:, :, hi])
+        project_half(acc0, x0, 1, (0, 1))
+        prepare("x0_woven0", wdq[1], lo, wd_raw[1][:])
+        project_half(acc0, x0, 0, (2, 3))
+        project_half(acc0, x0, 1, (2, 3))
+        for i in (0, 2, 1, 3):
+            gather(g2[0][:, i, :], i, 2 * J, wt2[:, lo])
+        prepare("x1_woven0", x1, lo, g1[:, :, lo])
+        project_half(acc1, x1, 0, range(NT))
+        prepare("x1_woven1", x1, hi, g1[:, :, hi])
+        project_half(acc1, x1, 1, range(NT))
+        for i in (0, 2, 1, 3):
+            gather(g2[1][:, i, :], i, 2 * J + HALF, wt2[:, hi])
+        prepare("x2_woven0", x2[0], lo, g2[0])
 
         r0 = [keep.tile([P, 2, J], F32, name="r0%d" % m) for m in range(2)]
         r1 = [keep.tile([P, 2, J], F32, name="r1%d" % m) for m in range(2)]
@@ -189,15 +185,12 @@ def tile_list_dl_relus_none_kernel(tc, xT, wgt, w4_words, w4_scales, wd, offs, o
         def add1(n):
             nc.vector.scalar_tensor_tensor(r1[n // 2][:, n % 2, :], acc1[n][:], 0.0, r0[n // 2][:, n % 2, :], MAX, ADD)
 
-        def project2(x2, banks):
+        def project2(x, banks):
             accs = []
             for m in range(2):
                 acc = psum.tile([P, 2, HALF], F32, name="acc2%d" % banks[m], tag="bank%d" % banks[m])
                 for u in range(2):
-                    for b in range(2):
-                        cols = slice(P * b, P * (b + 1))
-                        pass_w4(acc[:, u, cols], 2 * m + u, x2[1][:, cols], x2[2][:, cols], True, False)
-                        pass_wd(acc[:, u, cols], 2 * m + u, x2[1][:, cols], x2[2][:, cols], False, True)
+                    project(acc[:, u, :], 2 * m + u, x, 0, True, True)
                 accs.append(acc)
             return accs
 
@@ -212,19 +205,17 @@ def tile_list_dl_relus_none_kernel(tc, xT, wgt, w4_words, w4_scales, wd, offs, o
 
         relu0(0)
         relu0(1)
-        relu0(2)
-        acc2a = project2(x2a, (0, 1))
+        acc2a = project2(x2[0], (0, 1))
         add1(0)
         add1(1)
-        x2b = operand("x2b", HALF)
-        weave(x2b[0][:], g2b[:])
-        quantise(x2b[1][:], x2b[2][:], x2b[0][:])
-        acc2b = project2(x2b, (NT, NT + 1))
+        finish(acc2a[0], 0, 0)
+        prepare("x2_woven1", x2[1], lo, g2[1])
+        acc2b = project2(x2[1], (NT, NT + 1))
+        relu0(2)
         relu0(3)
         add1(2)
-        finish(acc2a[0], 0, 0, tag="x2b_woven")
         add1(3)
-        finish(acc2a[1], 1, 0)
         finish(acc2b[0], 0, 1)
+        finish(acc2a[1], 1, 0)
         finish(acc2b[1], 1, 1, slice(0, 1))
         finish(acc2b[1], 1, 1, slice(1, 2))

from contextlib import ExitStack

import concourse.mybir as mybir
from concourse.masks import make_identity

K, N, T, J = 512, 512, 2048, 512
PICKS = 3
FLOPS = 2 * 2 * PICKS * K * N * J

F32 = mybir.dt.float32
BF16 = mybir.dt.bfloat16
I32 = mybir.dt.int32
U32 = mybir.dt.uint32
U16 = mybir.dt.uint16
U8 = mybir.dt.uint8
FP8X4 = mybir.dt.float8_e4m3fn_x4
FP4X4 = mybir.dt.float4_e2m1fn_x4
MULT = mybir.AluOpType.mult
ADD = mybir.AluOpType.add
MAX = mybir.AluOpType.max
RELU = mybir.ActivationFunctionType.Relu
IDENTITY = mybir.ActivationFunctionType.Identity

P = 128
PACK = 4
HALF = J // 2
NT = N // P


def tile_list_dl_relus_none_kernel(tc, xT, wgt, w4_words, w4_scales, wd, offs, out):
    nc = tc.nc
    with ExitStack() as ctx:
        keep = ctx.enter_context(tc.tile_pool(name="keep", bufs=1))
        psum = ctx.enter_context(tc.psum_pool(name="psum", bufs=1))

        offsets = keep.tile([P, PICKS * J // 16], U16, name="offsets")
        planes = [keep.tile([P, T], F32, name="plane%d" % i) for i in range(PACK)]
        x_rows = xT.rearrange("(p i) t -> p i t", i=PACK)
        wd_rows = wd.rearrange("(p i) n -> p i n", i=PACK)

        w4_plane = keep.tile([P, N], U8, name="w4_plane", align_bytes=64)
        nc.vector.memset(w4_plane[:].bitcast(I32), 0)

        ident = keep.tile([P, P], F32, name="ident")
        make_identity(nc, ident[:])

        rows = keep.tile([P, P], F32, name="rows")
        nc.sync.dma_start(
            rows[:], wgt.rearrange("(g r) m -> g (r m)", r=16)[:, 0 : 16 * P].rearrange("g (b f) -> b g f", f=P)
        )
        nc.sync.dma_start(planes[0][:], x_rows[:, 0, :])
        nc.sync.dma_start(offsets[:], offs)
        wd_raw = [keep.tile([P, PACK, HALF], F32, name="wd_raw%d" % m) for m in range(2)]
        nc.sync.dma_start(planes[1][:], x_rows[:, 1, :])
        nc.sync.dma_start(planes[2][:], x_rows[:, 2, :])
        nc.sync.dma_start(wd_raw[0][:], wd_rows[:, :, 0:HALF])
        nc.sync.dma_start(planes[3][:], x_rows[:, 3, :])
        w4_codes = keep.tile([P, 2 * N], U8, name="w4_codes", align_bytes=64)
        nc.sync.dma_start(w4_codes[:].bitcast(I32), w4_words[0].bitcast(I32))
        for q in range(4):
            nc.sync.dma_start(w4_plane[32 * q : 32 * q + 4, :].bitcast(I32), w4_scales[0, 4 * q : 4 * q + 4, :].bitcast(I32))
        nc.sync.dma_start(wd_raw[1][:], wd_rows[:, :, HALF:N])

        turned = psum.tile([P, P], F32, name="turned", tag="bank7")
        nc.tensor.transpose(turned[:], rows[:], ident[:])

        def scalar_identity(dst, src):
            nc.scalar.activation(dst, src, IDENTITY)

        def spread(copy, dst, first, bank):
            blocks = dst.shape[1] // P
            wide = keep.tile([P, blocks * P], F32, name="wide%d" % bank, align_bytes=64)
            src = turned[:, first // 16 : first // 16 + 8 * blocks]
            copy(wide[:].rearrange("f (c r) -> f c r", r=16), src.unsqueeze(2).to_broadcast([P, 8 * blocks, 16]))
            back = psum.tile([P, blocks * P], F32, name="back%d" % bank, tag="bank%d" % bank)
            for b in range(blocks):
                nc.tensor.transpose(back[:, b * P : (b + 1) * P], wide[:, b * P : (b + 1) * P], ident[:])
            copy(dst, back[:])

        wt0 = keep.tile([P, J], F32, name="wt0", align_bytes=64)
        wt1 = keep.tile([P, J], F32, name="wt1")
        wt2 = keep.tile([P, J], F32, name="wt2")
        spread(nc.vector.tensor_copy, wt0[:, 0:HALF], 0, 0)
        spread(scalar_identity, wt0[:, HALF:J], HALF, 1)
        spread(nc.scalar.copy, wt1[:], J, 2)
        spread(nc.scalar.copy, wt2[:], 2 * J, 3)

        def gather(dst, i, first, weights):
            width = dst.shape[1]
            nc.vector.tensor_tensor(
                dst, planes[i][:].indirect(offsets[:, first // 16 : (first + width) // 16]), weights, MULT
            )

        def weave(dst, src):
            nc.scalar.copy(
                dst.rearrange("p (c i) t -> p c t i", i=4), src.rearrange("p t (c i) -> p c t i", i=4)
            )

        def quantise(codes, scales, woven):
            nc.vector.quantize_mx(out=codes.bitcast(FP8X4), scales=scales, in_=woven.rearrange("p j t -> p (j t)"))

        def operand(name, width, tag=None):
            codes = keep.tile([P, width], U32, name=name + "_codes", tag=tag or name + "_codes", align_bytes=64)
            scales = keep.tile([P, width], U8, name=name + "_scales", align_bytes=64)
            return codes, scales

        def prepare(name, dst, cols, src):
            woven = keep.tile([P, HALF, PACK], BF16, name=name, align_bytes=64)
            weave(woven[:], src)
            quantise(dst[0][:, cols], dst[1][:, cols], woven[:])

        lo, hi = slice(0, HALF), slice(HALF, J)
        stage0 = keep.tile([P, PACK * J], F32, name="stage0")
        stage1 = keep.tile([P, PACK * J], F32, name="stage1")
        g0 = stage0[:].rearrange("p (t j) -> p t j", t=PACK)
        g1 = stage1[:].rearrange("p (t j) -> p t j", t=PACK)
        g2 = [s[:, 0 : PACK * HALF].rearrange("p (t j) -> p t j", t=PACK) for s in (stage0, stage1)]
        x0, x1 = operand("x0", J), operand("x1", J)
        x2 = [operand("x2%d" % h, HALF) for h in range(2)]

        gather(g0[:, 0, lo], 0, 0, wt0[:, lo])
        gather(g0[:, 0, hi], 0, HALF, wt0[:, hi])
        gather(g1[:, 0, :], 0, J, wt1[:])
        for i in (1, 2):
            gather(g0[:, i, :], i, 0, wt0[:])
            gather(g1[:, i, :], i, J, wt1[:])
        wd_woven0 = keep.tile([P, HALF, PACK], BF16, name="wd_woven0", tag="wide3", align_bytes=64)
        weave(wd_woven0[:], wd_raw[0][:])
        gather(g0[:, 3, lo], 3, 0, wt0[:, lo])
        gather(g0[:, 3, hi], 3, HALF, wt0[:, hi])
        gather(g1[:, 3, :], 3, J, wt1[:])
        wdq = [operand("wd0", HALF, "wt0"), operand("wd1", HALF)]
        quantise(wdq[0][0][:], wdq[0][1][:], wd_woven0[:])

        def pass_w4(acc, n, codes, scales, start, stop):
            nc.tensor.matmul_mx(
                out=acc, lhsT=w4_codes[:, 2 * P * n : 2 * P * (n + 1)].bitcast(FP4X4), lhsT_scale=w4_plane[:, P * n : P * (n + 1)],
                rhs=codes.bitcast(FP8X4), rhs_scale=scales, start=start, stop=stop,
            )

        def pass_wd(acc, n, codes, scales, start, stop):
            cols = slice(P * (n % 2), P * (n % 2 + 1))
            nc.tensor.matmul_mx(
                out=acc, lhsT=wdq[n // 2][0][:, cols].bitcast(FP8X4), lhsT_scale=wdq[n // 2][1][:, cols],
                rhs=codes.bitcast(FP8X4), rhs_scale=scales, start=start, stop=stop,
            )

        acc0 = [psum.tile([P, J], F32, name="acc0%d" % n, tag="bank%d" % n) for n in range(NT)]
        acc1 = [psum.tile([P, J], F32, name="acc1%d" % n, tag="bank%d" % (NT + n)) for n in range(NT)]

        def project(acc, n, x, first, start, stop):
            cols = slice(first, first + HALF)
            pass_wd(acc, n, x[0][:, cols], x[1][:, cols], start, False)
            for b in range(2):
                cols = slice(first + P * b, first + P * (b + 1))
                pass_w4(acc[:, P * b : P * (b + 1)], n, x[0][:, cols], x[1][:, cols], False, stop and b == 1)

        def project_half(accs, x, h, tiles):
            for n in tiles:
                project(accs[n][:, h * HALF : (h + 1) * HALF], n, x, h * HALF, h == 0, h == 1)

        prepare("x0_woven0", x0, lo, g0[:, :, lo])
        project_half(acc0, x0, 0, (0, 1))
        prepare("x0_woven1", x0, hi, g0[:, :, hi])
        project_half(acc0, x0, 1, (0, 1))
        prepare("x0_woven0", wdq[1], lo, wd_raw[1][:])
        project_half(acc0, x0, 0, (2, 3))
        project_half(acc0, x0, 1, (2, 3))
        for i in (0, 2, 1, 3):
            gather(g2[0][:, i, :], i, 2 * J, wt2[:, lo])
        prepare("x1_woven0", x1, lo, g1[:, :, lo])
        project_half(acc1, x1, 0, range(NT))
        prepare("x1_woven1", x1, hi, g1[:, :, hi])
        project_half(acc1, x1, 1, range(NT))
        for i in (0, 2, 1, 3):
            gather(g2[1][:, i, :], i, 2 * J + HALF, wt2[:, hi])
        prepare("x2_woven0", x2[0], lo, g2[0])

        r0 = [keep.tile([P, 2, J], F32, name="r0%d" % m) for m in range(2)]
        r1 = [keep.tile([P, 2, J], F32, name="r1%d" % m) for m in range(2)]

        def relu0(n):
            nc.scalar.activation(r0[n // 2][:, n % 2, :], acc0[n][:], RELU)

        def add1(n):
            nc.vector.scalar_tensor_tensor(r1[n // 2][:, n % 2, :], acc1[n][:], 0.0, r0[n // 2][:, n % 2, :], MAX, ADD)

        def project2(x, banks):
            accs = []
            for m in range(2):
                acc = psum.tile([P, 2, HALF], F32, name="acc2%d" % banks[m], tag="bank%d" % banks[m])
                for u in range(2):
                    project(acc[:, u, :], 2 * m + u, x, 0, True, True)
                accs.append(acc)
            return accs

        out_rows = out.rearrange("(m u p) j -> p m u j", p=P, u=2)

        def finish(acc, m, h, tiles=slice(0, 2), tag=None):
            cols = slice(h * HALF, (h + 1) * HALF)
            name = "res%d%d%d" % (m, h, tiles.start)
            res = keep.tile([P, tiles.stop - tiles.start, HALF], F32, name=name, tag=tag or name, align_bytes=64)
            nc.vector.scalar_tensor_tensor(res[:], acc[:, tiles, :], 0.0, r1[m][:, tiles, cols], MAX, ADD)
            nc.sync.dma_start(out_rows[:, m, tiles, cols], res[:])

        relu0(0)
        relu0(1)
        acc2a = project2(x2[0], (0, 1))
        add1(0)
        add1(1)
        finish(acc2a[0], 0, 0)
        prepare("x2_woven1", x2[1], lo, g2[1])
        acc2b = project2(x2[1], (NT, NT + 1))
        relu0(2)
        relu0(3)
        add1(2)
        add1(3)
        finish(acc2b[0], 0, 1)
        finish(acc2a[1], 1, 0)
        finish(acc2b[1], 1, 1, slice(0, 1))
        finish(acc2b[1], 1, 1, slice(1, 2))
